import numpy as np
import ml_dtypes


def mxq(x, axis, fmt="e4m3"):
    dtype, down = {"e4m3": (ml_dtypes.float8_e4m3fn, 7), "e5m2": (ml_dtypes.float8_e5m2, 14)}[fmt]
    v = np.moveaxis(np.asarray(x, np.float32).astype(ml_dtypes.bfloat16).astype(np.float64), axis, -1)
    blocks = v.reshape(v.shape[:-1] + (-1, 32))
    amax = np.abs(blocks).max(-1, keepdims=True)
    byte = np.maximum(np.where(amax > 0, np.frexp(amax)[1] - 1 + 127, 0) - down, 1)
    scale = np.exp2(byte - 127.0)
    codes = (blocks / scale).astype(np.float32).astype(dtype).astype(np.float64)
    return np.moveaxis((codes * scale).reshape(v.shape), -1, axis)


WIDE = False


def mx_kscale(k):
    if not WIDE:
        return np.ones(k)
    levels = np.array([10, -10, 5, -5, 0])
    if k % 512:
        return np.exp2(np.random.permutation(np.resize(levels, k // 32))).repeat(32)
    a = np.empty((k // 512, 16))
    for p in range(k // 512):
        a[p, :8] = np.random.permutation(np.resize(levels, 8))
        for g in range(8):
            far = levels[np.abs(levels - a[p, g]) >= 10]
            a[p, g + 8] = far[np.random.randint(len(far))]
    return np.exp2(a.ravel()).repeat(32)


def f64(x):
    return np.asarray(x).astype(np.float64)


def striped(idx):
    return np.tile(idx.reshape(-1, 16).T, (8, 1)).astype(np.uint16)


def unstriped(offs):
    return offs[:16].T.reshape(-1).astype(np.int64)


def pack_weight(w):
    k, n = w.shape
    w = f64(np.asarray(w, np.float32).astype(ml_dtypes.bfloat16)).reshape(k // 32, 32, n)
    amax = np.abs(w).max(1)
    byte = np.clip(np.where(amax > 0, np.frexp(amax)[1] - 1 + 127 - 7, 1), 1, 254)
    scaled = (w * np.exp2(127.0 - byte)[:, None, :]).reshape(k, n).astype(np.float32)
    words = np.ascontiguousarray(scaled.reshape(k // 512, 128, 4, n).transpose(0, 1, 3, 2)).astype(ml_dtypes.float8_e4m3fn).view(np.uint8)
    return words, np.ascontiguousarray(byte.astype(np.uint8).reshape(k // 512, 16, n))


def unpack_weight(words, scales):
    g, p, n, _ = words.shape
    vals = np.ascontiguousarray(words).view(ml_dtypes.float8_e4m3fn).astype(np.float64) * np.repeat(np.exp2(scales.astype(np.float64) - 127.0), 8, axis=1)[..., None]
    return vals.transpose(0, 1, 3, 2).reshape(g * 512, n)


K, T, E, C, N = 1024, 512, 8, 128, 256


def by_expert(wq, xq):
    return np.concatenate([wq[e].T @ xq[:, e * C:(e + 1) * C] for e in range(E)], axis=1)


def setup_inputs():
    n = np.random.standard_normal
    s = mx_kscale(K)[:, None]
    first = np.random.permutation(np.repeat(np.arange(E), T // E))
    second = (first + 1 + np.random.permutation(np.repeat(np.arange(E - 1), -(-T // (E - 1)))[:T])) % E
    while np.bincount(second, minlength=E).max() != T // E:
        load = np.bincount(second, minlength=E); hi, lo = int(load.argmax()), int(load.argmin())
        t = np.flatnonzero((second == hi) & (first != lo))[0]; second[t] = lo
    slot_token = np.empty(E * C, np.int64); pos = np.empty((2, T), np.int64); fill = np.zeros(E, np.int64)
    place = np.stack([np.random.permutation(C) for _ in range(E)])
    for r, deal in enumerate((first, second)):
        for t in np.random.permutation(T):
            e = deal[t]; j = e * C + place[e, fill[e]]; fill[e] += 1; slot_token[j] = t; pos[r, t] = j
    g = np.random.uniform(0.2, 0.8, T)
    packed = [pack_weight(m) for m in n((E, K, N)) / np.sqrt(K) / s[None]]
    return {
        "xT": (n((K, T)) * s).astype(np.float32),
        "w_words": np.stack([m[0] for m in packed]),
        "w_scales": np.stack([m[1] for m in packed]),
        "gate": np.stack([np.tile(g, (N, 1)), np.tile(1.0 - g, (N, 1))]).astype(np.float32),
        "offs": striped(slot_token),
        "pos1": striped(pos[0]),
        "pos2": striped(pos[1]),
    }


def reference(xT, w_words, w_scales, gate, offs, pos1, pos2):
    idx = unstriped(offs)
    xq = mxq(f64(xT)[:, idx], 0, "e4m3")
    w = np.stack([unpack_weight(w_words[e], w_scales[e]) for e in range(E)])
    y = by_expert(w, xq)
    return f64(gate[0]) * y[:, unstriped(pos1)] + f64(gate[1]) * y[:, unstriped(pos2)]

@@ -1,0 +1,151 @@
+from contextlib import ExitStack
+
+import concourse.mybir as mybir
+from concourse.masks import make_identity
+
+K, T, E, C, N = 1024, 512, 8, 128, 256
+P = 128
+PASSES = K // 512
+SLOTS = E * C
+HALF = T // 2
+WINDOW = 1536
+FLOPS = 2 * K * N * SLOTS
+
+F32 = mybir.dt.float32
+BF16 = mybir.dt.bfloat16
+I32 = mybir.dt.int32
+U32 = mybir.dt.uint32
+U16 = mybir.dt.uint16
+U8 = mybir.dt.uint8
+FP8X4 = mybir.dt.float8_e4m3fn_x4
+MULT = mybir.AluOpType.mult
+ADD = mybir.AluOpType.add
+
+SLICES = [(0, 512), (512, 896), (896, 1024)]
+SPLIT = 96
+
+
+def tile_routed_moe_kernel(tc, xT, w_words, w_scales, gate, offs, pos1, pos2, out):
+    nc = tc.nc
+    x_rows = xT.rearrange("(a p j) t -> a p j t", p=P, j=4)
+    w_rows = w_words.rearrange("e a p n r -> p (e a) (n r)")
+    ws_rows = w_scales.rearrange("e a q n -> q (e a) n")
+
+    with ExitStack() as ctx:
+        lists = ctx.enter_context(tc.tile_pool(name="lists", bufs=1))
+        keep = ctx.enter_context(tc.tile_pool(name="keep", bufs=1))
+        psum = ctx.enter_context(tc.psum_pool(name="psum", bufs=1))
+
+        offs_t = lists.tile([P, SLOTS // 16], U16, name="offs_t")
+        pos1_t = lists.tile([P, T // 16], U16, name="pos1_t")
+        pos2_t = lists.tile([P, T // 16], U16, name="pos2_t")
+
+        codes = [keep.tile([P, WINDOW], I32, name=f"codes{a}", align_bytes=64) for a in range(PASSES)]
+        scales = keep.tile([P, WINDOW], U8, name="scales", align_bytes=64)
+        ws = keep.tile([P, E * PASSES, N], U8, name="ws", align_bytes=64)
+        nc.gpsimd.memset(scales[:], 0)
+        nc.gpsimd.memset(ws[:].rearrange("p g n -> p (g n)").bitcast(I32), 0)
+        ident = keep.tile([P, P], F32, name="ident")
+        make_identity(nc, ident[:])
+        for a in range(PASSES):
+            nc.vector.memset(codes[a][:, T:], 0)
+
+        raw = {}
+        for a in range(PASSES):
+            for h in range(2):
+                raw[a, h] = keep.tile([P, 4, HALF], F32, name=f"raw{a}{h}")
+                nc.sync.dma_start(raw[a, h][:], x_rows[a, :, :, h * HALF : (h + 1) * HALF])
+            if a == 0:
+                nc.sync.dma_start(offs_t[:], offs)
+        for q in range(4):
+            nc.sync.dma_start(ws[32 * q : 32 * q + 4, :, :].bitcast(I32), ws_rows[4 * q : 4 * q + 4].bitcast(I32))
+        ww = []
+        for h in range(2):
+            w_t = keep.tile([P, E * PASSES // 2, N], I32, name=f"ww{h}", align_bytes=64)
+            nc.sync.dma_start(w_t[:], w_rows[:, 8 * h : 8 * h + 8, :].bitcast(I32))
+            ww.append(w_t)
+        nc.sync.dma_start(pos1_t[:], pos1)
+        nc.sync.dma_start(pos2_t[:], pos2)
+        gates = []
+        for b in range(2):
+            g_t = keep.tile([P, 2, T], F32, name=f"gate{b}")
+            nc.sync.dma_start(g_t[:], gate[:, b * P : (b + 1) * P, :].rearrange("r p t -> p r t"))
+            gates.append(g_t)
+
+        grouped = {}
+
+        def cast(a, h):
+            g = keep.tile([P, HALF, 4], BF16, name=f"grouped{a}{h}", align_bytes=64)
+            grouped[a, h] = g
+            src = raw[a, h][:].rearrange("p j t -> p t j")
+            if a == 0:
+                nc.scalar.copy(g[:, :SPLIT, :], src[:, :SPLIT, :])
+                nc.vector.tensor_copy(g[:, SPLIT:, :], src[:, SPLIT:, :])
+            else:
+                nc.scalar.copy(g[:], src)
+
+        def quantize(a, h):
+            cols = slice(h * HALF, (h + 1) * HALF)
+            nc.vector.quantize_mx(
+                out=codes[a][:, cols].bitcast(FP8X4),
+                scales=scales[4 * a : P, cols],
+                in_=grouped[a, h][:].rearrange("p t j -> p (t j)"),
+            )
+
+        cast(0, 0)
+        cast(0, 1)
+        quantize(0, 0)
+        quantize(0, 1)
+        words0 = keep.tile([P, SLOTS], I32, name="words0", align_bytes=64)
+        nc.vector.tensor_copy(words0[:].bitcast(U32), codes[0][:].bitcast(U32).indirect(offs_t[:]))
+        cast(1, 0)
+        cast(1, 1)
+        quantize(1, 0)
+        quantize(1, 1)
+
+        y = [keep.tile([P, SLOTS], F32, name=f"y{b}") for b in range(2)]
+        for lo, hi in SLICES:
+            n = hi - lo
+            window = 1024 if n > 128 else 512
+            entries = offs_t[:, lo // 16 : hi // 16]
+            byte_t = keep.tile([P, n], U8, name=f"bytes{lo}", align_bytes=64)
+            words1 = keep.tile([P, n], I32, name=f"words1_{lo}", align_bytes=64)
+            nc.vector.tensor_copy(byte_t[:], scales[:, :window].indirect(entries))
+            nc.vector.tensor_copy(words1[:].bitcast(U32), codes[1][:, :window].bitcast(U32).indirect(entries))
+            for b in range(2):
+                acc = psum.tile([P, n], F32, name=f"acc{b}_{lo}")
+                for e in range(lo // C, hi // C):
+                    here = slice(e * C - lo, (e + 1) * C - lo)
+                    for a in range(PASSES):
+                        words = words0[:, e * C : (e + 1) * C] if a == 0 else words1[:, here]
+                        nc.tensor.matmul_mx(
+                            out=acc[:, here],
+                            lhsT=ww[e // 4][:, (e % 4) * PASSES + a, b * P : (b + 1) * P].bitcast(FP8X4),
+                            lhsT_scale=ws[:, e * PASSES + a, b * P : (b + 1) * P],
+                            rhs=words.bitcast(FP8X4),
+                            rhs_scale=byte_t[4 * a : P, here],
+                            start=(a == 0),
+                            stop=(a == PASSES - 1),
+                        )
+                nc.scalar.copy(y[b][:, lo:hi], acc[:])
+
+        first = [keep.tile([P, T], F32, name=f"first{b}") for b in range(2)]
+        second = [keep.tile([P, T], F32, name=f"second{b}") for b in range(2)]
+        nc.vector.tensor_tensor(first[0][:], y[0][:].indirect(pos1_t[:]), gates[0][:, 0, :], MULT)
+        nc.vector.tensor_tensor(second[0][:], y[0][:].indirect(pos2_t[:]), gates[0][:, 1, :], MULT)
+        nc.vector.tensor_tensor(first[1][:], y[1][:].indirect(pos1_t[:]), gates[1][:, 0, :], MULT)
+        both = psum.tile([P, T], F32, name="both")
+        nc.tensor.matmul(both[:], ident[:], first[0][:], start=True, stop=False)
+        nc.tensor.matmul(both[:], ident[:], second[0][:], start=False, stop=True)
+        out0 = keep.tile([P, T], F32, name="out0")
+        nc.scalar.copy(out0[:], both[:])
+        nc.sync.dma_start(out[:P, :], out0[:])
+        for h in range(2):
+            cols = slice(h * HALF, (h + 1) * HALF)
+            nc.vector.tensor_tensor(
+                second[1][:, cols], y[1][:].indirect(pos2_t[:, h * HALF // 16 : (h + 1) * HALF // 16]), gates[1][:, 1, cols], MULT
+            )
+        for h in range(2):
+            cols = slice(h * HALF, (h + 1) * HALF)
+            nc.vector.tensor_tensor(second[1][:, cols], first[1][:, cols], second[1][:, cols], ADD)
+            nc.sync.dma_start(out[P:, cols], second[1][:, cols])

@@ -1,7 +1,6 @@
 from contextlib import ExitStack
 
 import concourse.mybir as mybir
-from concourse.masks import make_identity
 
 K, T, E, C, N = 1024, 512, 8, 128, 256
 P = 128
@@ -22,7 +21,7 @@ MULT = mybir.AluOpType.mult
 ADD = mybir.AluOpType.add
 
 SLICES = [(0, 512), (512, 896), (896, 1024)]
-SPLIT = 96
+SCALAR_TOKENS = [160, 368]
 
 
 def tile_routed_moe_kernel(tc, xT, w_words, w_scales, gate, offs, pos1, pos2, out):
@@ -43,18 +42,16 @@ def tile_routed_moe_kernel(tc, xT, w_words, w_scales, gate, offs, pos1, pos2, ou
         codes = [keep.tile([P, WINDOW], I32, name=f"codes{a}", align_bytes=64) for a in range(PASSES)]
         scales = keep.tile([P, WINDOW], U8, name="scales", align_bytes=64)
         ws = keep.tile([P, E * PASSES, N], U8, name="ws", align_bytes=64)
-        nc.gpsimd.memset(scales[:], 0)
+        nc.gpsimd.memset(scales[:].bitcast(I32), 0)
         nc.gpsimd.memset(ws[:].rearrange("p g n -> p (g n)").bitcast(I32), 0)
-        ident = keep.tile([P, P], F32, name="ident")
-        make_identity(nc, ident[:])
         for a in range(PASSES):
             nc.vector.memset(codes[a][:, T:], 0)
 
-        raw = {}
+        raw = []
         for a in range(PASSES):
-            for h in range(2):
-                raw[a, h] = keep.tile([P, 4, HALF], F32, name=f"raw{a}{h}")
-                nc.sync.dma_start(raw[a, h][:], x_rows[a, :, :, h * HALF : (h + 1) * HALF])
+            r_t = keep.tile([P, 4, T], F32, name=f"raw{a}")
+            nc.sync.dma_start(r_t[:], x_rows[a])
+            raw.append(r_t)
             if a == 0:
                 nc.sync.dma_start(offs_t[:], offs)
         for q in range(4):
@@ -72,34 +69,29 @@ def tile_routed_moe_kernel(tc, xT, w_words, w_scales, gate, offs, pos1, pos2, ou
             nc.sync.dma_start(g_t[:], gate[:, b * P : (b + 1) * P, :].rearrange("r p t -> p r t"))
             gates.append(g_t)
 
-        grouped = {}
+        grouped = [keep.tile([P, T, 4], BF16, name=f"grouped{a}", align_bytes=64) for a in range(PASSES)]
 
-        def cast(a, h):
-            g = keep.tile([P, HALF, 4], BF16, name=f"grouped{a}{h}", align_bytes=64)
-            grouped[a, h] = g
-            src = raw[a, h][:].rearrange("p j t -> p t j")
-            if a == 0:
-                nc.scalar.copy(g[:, :SPLIT, :], src[:, :SPLIT, :])
-                nc.vector.tensor_copy(g[:, SPLIT:, :], src[:, SPLIT:, :])
-            else:
-                nc.scalar.copy(g[:], src)
+        def cast(copy, a, lo, hi):
+            copy(grouped[a][:, lo:hi, :], raw[a][:].rearrange("p j t -> p t j")[:, lo:hi, :])
 
         def quantize(a, h):
             cols = slice(h * HALF, (h + 1) * HALF)
             nc.vector.quantize_mx(
                 out=codes[a][:, cols].bitcast(FP8X4),
                 scales=scales[4 * a : P, cols],
-                in_=grouped[a, h][:].rearrange("p t j -> p (t j)"),
+                in_=grouped[a][:, cols, :].rearrange("p t j -> p (t j)"),
             )
 
-        cast(0, 0)
-        cast(0, 1)
-        quantize(0, 0)
+        cast(nc.scalar.copy, 0, 0, SCALAR_TOKENS[0])
+        cast(nc.vector.tensor_copy, 0, HALF, T)
+        cast(nc.vector.tensor_copy, 0, SCALAR_TOKENS[0], HALF)
         quantize(0, 1)
+        quantize(0, 0)
         words0 = keep.tile([P, SLOTS], I32, name="words0", align_bytes=64)
         nc.vector.tensor_copy(words0[:].bitcast(U32), codes[0][:].bitcast(U32).indirect(offs_t[:]))
-        cast(1, 0)
-        cast(1, 1)
+        cast(nc.scalar.copy, 1, 0, HALF)
+        cast(nc.scalar.copy, 1, HALF, SCALAR_TOKENS[1])
+        cast(nc.vector.tensor_copy, 1, SCALAR_TOKENS[1], T)
         quantize(1, 0)
         quantize(1, 1)
 
@@ -134,12 +126,8 @@ def tile_routed_moe_kernel(tc, xT, w_words, w_scales, gate, offs, pos1, pos2, ou
         nc.vector.tensor_tensor(first[0][:], y[0][:].indirect(pos1_t[:]), gates[0][:, 0, :], MULT)
         nc.vector.tensor_tensor(second[0][:], y[0][:].indirect(pos2_t[:]), gates[0][:, 1, :], MULT)
         nc.vector.tensor_tensor(first[1][:], y[1][:].indirect(pos1_t[:]), gates[1][:, 0, :], MULT)
-        both = psum.tile([P, T], F32, name="both")
-        nc.tensor.matmul(both[:], ident[:], first[0][:], start=True, stop=False)
-        nc.tensor.matmul(both[:], ident[:], second[0][:], start=False, stop=True)
-        out0 = keep.tile([P, T], F32, name="out0")
-        nc.scalar.copy(out0[:], both[:])
-        nc.sync.dma_start(out[:P, :], out0[:])
+        nc.vector.tensor_tensor(second[0][:], first[0][:], second[0][:], ADD)
+        nc.sync.dma_start(out[:P, :], second[0][:])
         for h in range(2):
             cols = slice(h * HALF, (h + 1) * HALF)
             nc.vector.tensor_tensor(

@@ -1,6 +1,7 @@
 from contextlib import ExitStack
 
 import concourse.mybir as mybir
+from concourse.masks import make_identity
 
 K, T, E, C, N = 1024, 512, 8, 128, 256
 P = 128
@@ -20,8 +21,7 @@ FP8X4 = mybir.dt.float8_e4m3fn_x4
 MULT = mybir.AluOpType.mult
 ADD = mybir.AluOpType.add
 
-SLICES = [(0, 512), (512, 896), (896, 1024)]
-SCALAR_TOKENS = [160, 368]
+SCALAR_TOKENS = [168, 368]
 
 
 def tile_routed_moe_kernel(tc, xT, w_words, w_scales, gate, offs, pos1, pos2, out):
@@ -33,7 +33,7 @@ def tile_routed_moe_kernel(tc, xT, w_words, w_scales, gate, offs, pos1, pos2, ou
     with ExitStack() as ctx:
         lists = ctx.enter_context(tc.tile_pool(name="lists", bufs=1))
         keep = ctx.enter_context(tc.tile_pool(name="keep", bufs=1))
-        psum = ctx.enter_context(tc.psum_pool(name="psum", bufs=1))
+        psum = ctx.enter_context(tc.psum_pool(name="psum", bufs=8))
 
         offs_t = lists.tile([P, SLOTS // 16], U16, name="offs_t")
         pos1_t = lists.tile([P, T // 16], U16, name="pos1_t")
@@ -44,6 +44,8 @@ def tile_routed_moe_kernel(tc, xT, w_words, w_scales, gate, offs, pos1, pos2, ou
         ws = keep.tile([P, E * PASSES, N], U8, name="ws", align_bytes=64)
         nc.gpsimd.memset(scales[:].bitcast(I32), 0)
         nc.gpsimd.memset(ws[:].rearrange("p g n -> p (g n)").bitcast(I32), 0)
+        ident = keep.tile([P, P], F32, name="ident")
+        make_identity(nc, ident[:])
         for a in range(PASSES):
             nc.vector.memset(codes[a][:, T:], 0)
 
@@ -57,82 +59,114 @@ def tile_routed_moe_kernel(tc, xT, w_words, w_scales, gate, offs, pos1, pos2, ou
         for q in range(4):
             nc.sync.dma_start(ws[32 * q : 32 * q + 4, :, :].bitcast(I32), ws_rows[4 * q : 4 * q + 4].bitcast(I32))
         ww = []
-        for h in range(2):
-            w_t = keep.tile([P, E * PASSES // 2, N], I32, name=f"ww{h}", align_bytes=64)
-            nc.sync.dma_start(w_t[:], w_rows[:, 8 * h : 8 * h + 8, :].bitcast(I32))
+        for h in range(4):
+            w_t = keep.tile([P, E * PASSES // 4, N], I32, name=f"ww{h}", align_bytes=64)
+            nc.sync.dma_start(w_t[:], w_rows[:, 4 * h : 4 * h + 4, :].bitcast(I32))
             ww.append(w_t)
         nc.sync.dma_start(pos1_t[:], pos1)
         nc.sync.dma_start(pos2_t[:], pos2)
-        gates = []
+        gates = {}
         for b in range(2):
-            g_t = keep.tile([P, 2, T], F32, name=f"gate{b}")
-            nc.sync.dma_start(g_t[:], gate[:, b * P : (b + 1) * P, :].rearrange("r p t -> p r t"))
-            gates.append(g_t)
+            for r in range(2):
+                g_t = keep.tile([P, T], F32, name=f"gate{r}{b}")
+                nc.sync.dma_start(g_t[:], gate[r, b * P : (b + 1) * P, :])
+                gates[r, b] = g_t
 
         grouped = [keep.tile([P, T, 4], BF16, name=f"grouped{a}", align_bytes=64) for a in range(PASSES)]
 
         def cast(copy, a, lo, hi):
             copy(grouped[a][:, lo:hi, :], raw[a][:].rearrange("p j t -> p t j")[:, lo:hi, :])
 
-        def quantize(a, h):
-            cols = slice(h * HALF, (h + 1) * HALF)
+        def quantize(a, lo, hi):
             nc.vector.quantize_mx(
-                out=codes[a][:, cols].bitcast(FP8X4),
-                scales=scales[4 * a : P, cols],
-                in_=grouped[a][:, cols, :].rearrange("p t j -> p (t j)"),
+                out=codes[a][:, lo:hi].bitcast(FP8X4),
+                scales=scales[4 * a : P, lo:hi],
+                in_=grouped[a][:, lo:hi, :].rearrange("p t j -> p (t j)"),
             )
 
         cast(nc.scalar.copy, 0, 0, SCALAR_TOKENS[0])
         cast(nc.vector.tensor_copy, 0, HALF, T)
         cast(nc.vector.tensor_copy, 0, SCALAR_TOKENS[0], HALF)
-        quantize(0, 1)
-        quantize(0, 0)
+        quantize(0, HALF, T)
+        quantize(0, 0, HALF)
         words0 = keep.tile([P, SLOTS], I32, name="words0", align_bytes=64)
         nc.vector.tensor_copy(words0[:].bitcast(U32), codes[0][:].bitcast(U32).indirect(offs_t[:]))
         cast(nc.scalar.copy, 1, 0, HALF)
         cast(nc.scalar.copy, 1, HALF, SCALAR_TOKENS[1])
         cast(nc.vector.tensor_copy, 1, SCALAR_TOKENS[1], T)
-        quantize(1, 0)
-        quantize(1, 1)
+        quantize(1, 0, HALF)
+        quantize(1, HALF, T)
 
         y = [keep.tile([P, SLOTS], F32, name=f"y{b}") for b in range(2)]
-        for lo, hi in SLICES:
-            n = hi - lo
-            window = 1024 if n > 128 else 512
-            entries = offs_t[:, lo // 16 : hi // 16]
-            byte_t = keep.tile([P, n], U8, name=f"bytes{lo}", align_bytes=64)
-            words1 = keep.tile([P, n], I32, name=f"words1_{lo}", align_bytes=64)
-            nc.vector.tensor_copy(byte_t[:], scales[:, :window].indirect(entries))
-            nc.vector.tensor_copy(words1[:].bitcast(U32), codes[1][:, :window].bitcast(U32).indirect(entries))
+        byte_t = keep.tile([P, SLOTS], U8, name="byte_t", align_bytes=64)
+        words1 = keep.tile([P, SLOTS], I32, name="words1", align_bytes=64)
+
+        def gather(dst, src, lo, hi):
+            window = 1024 if hi - lo > 256 else 512
+            nc.vector.tensor_copy(dst[:, lo:hi], src[:, :window].indirect(offs_t[:, lo // 16 : hi // 16]))
+
+        def multiply(acc, c0, e, b, a):
+            slots = slice(e * C, (e + 1) * C)
+            words = words0 if a == 0 else words1
+            nc.tensor.matmul_mx(
+                out=acc[:, c0 : c0 + C],
+                lhsT=ww[e // 2][:, (e % 2) * PASSES + a, b * P : (b + 1) * P].bitcast(FP8X4),
+                lhsT_scale=ws[:, e * PASSES + a, b * P : (b + 1) * P],
+                rhs=words[:, slots].bitcast(FP8X4),
+                rhs_scale=byte_t[4 * a : P, slots],
+                start=(a == 0),
+                stop=(a == PASSES - 1),
+            )
+
+        u_words1 = words1[:].bitcast(U32)
+        u_codes1 = codes[1][:].bitcast(U32)
+        acc = {}
+
+        def open_groups(experts):
+            for e in experts:
+                for b in range(2):
+                    acc_t = psum.tile([P, C], F32, name="acc")
+                    multiply(acc_t, 0, e, b, 0)
+                    acc[e, b] = acc_t
+
+        def close_groups(experts):
             for b in range(2):
-                acc = psum.tile([P, n], F32, name=f"acc{b}_{lo}")
-                for e in range(lo // C, hi // C):
-                    here = slice(e * C - lo, (e + 1) * C - lo)
-                    for a in range(PASSES):
-                        words = words0[:, e * C : (e + 1) * C] if a == 0 else words1[:, here]
-                        nc.tensor.matmul_mx(
-                            out=acc[:, here],
-                            lhsT=ww[e // 4][:, (e % 4) * PASSES + a, b * P : (b + 1) * P].bitcast(FP8X4),
-                            lhsT_scale=ws[:, e * PASSES + a, b * P : (b + 1) * P],
-                            rhs=words.bitcast(FP8X4),
-                            rhs_scale=byte_t[4 * a : P, here],
-                            start=(a == 0),
-                            stop=(a == PASSES - 1),
-                        )
-                nc.scalar.copy(y[b][:, lo:hi], acc[:])
+                for e in experts:
+                    multiply(acc[e, b], 0, e, b, 1)
+                    nc.scalar.copy(y[b][:, e * C : (e + 1) * C], acc[e, b][:])
+
+        gather(byte_t, scales, 0, 512)
+        open_groups(range(0, 4))
+        gather(u_words1, u_codes1, 0, 256)
+        close_groups(range(0, 2))
+        gather(u_words1, u_codes1, 256, 512)
+        close_groups(range(2, 4))
+        gather(byte_t, scales, 512, 1024)
+        open_groups(range(4, 6))
+        gather(u_words1, u_codes1, 512, 768)
+        close_groups(range(4, 6))
+        gather(u_words1, u_codes1, 768, 1024)
+        for b in range(2):
+            acc_t = psum.tile([P, 2 * C], F32, name="acc")
+            for e in (6, 7):
+                for a in range(PASSES):
+                    multiply(acc_t, (e - 6) * C, e, b, a)
+            nc.scalar.copy(y[b][:, 6 * C :], acc_t[:])
 
         first = [keep.tile([P, T], F32, name=f"first{b}") for b in range(2)]
         second = [keep.tile([P, T], F32, name=f"second{b}") for b in range(2)]
-        nc.vector.tensor_tensor(first[0][:], y[0][:].indirect(pos1_t[:]), gates[0][:, 0, :], MULT)
-        nc.vector.tensor_tensor(second[0][:], y[0][:].indirect(pos2_t[:]), gates[0][:, 1, :], MULT)
-        nc.vector.tensor_tensor(first[1][:], y[1][:].indirect(pos1_t[:]), gates[1][:, 0, :], MULT)
-        nc.vector.tensor_tensor(second[0][:], first[0][:], second[0][:], ADD)
-        nc.sync.dma_start(out[:P, :], second[0][:])
-        for h in range(2):
-            cols = slice(h * HALF, (h + 1) * HALF)
-            nc.vector.tensor_tensor(
-                second[1][:, cols], y[1][:].indirect(pos2_t[:, h * HALF // 16 : (h + 1) * HALF // 16]), gates[1][:, 1, cols], MULT
-            )
+        both = psum.tile([P, 256], F32, name="both", tag="acc")
+        summed = keep.tile([P, 256], F32, name="summed")
+        for b in range(2):
+            nc.vector.tensor_tensor(first[b][:], y[b][:].indirect(pos1_t[:]), gates[0, b][:], MULT)
+            nc.vector.tensor_tensor(second[b][:], y[b][:].indirect(pos2_t[:]), gates[1, b][:], MULT)
+            if b == 0:
+                nc.tensor.matmul(both[:], ident[:], first[0][:, :256], start=True, stop=False)
+                nc.tensor.matmul(both[:], ident[:], second[0][:, :256], start=False, stop=True)
+                nc.scalar.copy(summed[:], both[:])
+                nc.sync.dma_start(out[:P, :256], summed[:])
+        nc.vector.tensor_tensor(second[0][:, 256:], first[0][:, 256:], second[0][:, 256:], ADD)
+        nc.sync.dma_start(out[:P, 256:], second[0][:, 256:])
         for h in range(2):
             cols = slice(h * HALF, (h + 1) * HALF)
             nc.vector.tensor_tensor(second[1][:, cols], first[1][:, cols], second[1][:, cols], ADD)

@@ -21,14 +21,14 @@ FP8X4 = mybir.dt.float8_e4m3fn_x4
 MULT = mybir.AluOpType.mult
 ADD = mybir.AluOpType.add
 
-SCALAR_TOKENS = [168, 368]
+SCALAR_TOKENS = [168]
 
 
 def tile_routed_moe_kernel(tc, xT, w_words, w_scales, gate, offs, pos1, pos2, out):
     nc = tc.nc
     x_rows = xT.rearrange("(a p j) t -> a p j t", p=P, j=4)
     w_rows = w_words.rearrange("e a p n r -> p (e a) (n r)")
-    ws_rows = w_scales.rearrange("e a q n -> q (e a) n")
+    ws_rows = w_scales.rearrange("e a (q r) n -> r q (e a) n", r=4)
 
     with ExitStack() as ctx:
         lists = ctx.enter_context(tc.tile_pool(name="lists", bufs=1))
@@ -52,12 +52,16 @@ def tile_routed_moe_kernel(tc, xT, w_words, w_scales, gate, offs, pos1, pos2, ou
         raw = []
         for a in range(PASSES):
             r_t = keep.tile([P, 4, T], F32, name=f"raw{a}")
-            nc.sync.dma_start(r_t[:], x_rows[a])
+            if a == 0:
+                nc.sync.dma_start(r_t[:], x_rows[a])
+            else:
+                for h in range(2):
+                    nc.sync.dma_start(r_t[:, :, h * HALF : (h + 1) * HALF], x_rows[a, :, :, h * HALF : (h + 1) * HALF])
             raw.append(r_t)
             if a == 0:
                 nc.sync.dma_start(offs_t[:], offs)
-        for q in range(4):
-            nc.sync.dma_start(ws[32 * q : 32 * q + 4, :, :].bitcast(I32), ws_rows[4 * q : 4 * q + 4].bitcast(I32))
+        for r in range(4):
+            nc.sync.dma_start(ws[r:P:32, :, :].bitcast(I32), ws_rows[r].bitcast(I32))
         ww = []
         for h in range(4):
             w_t = keep.tile([P, E * PASSES // 4, N], I32, name=f"ww{h}", align_bytes=64)
@@ -75,7 +79,10 @@ def tile_routed_moe_kernel(tc, xT, w_words, w_scales, gate, offs, pos1, pos2, ou
         grouped = [keep.tile([P, T, 4], BF16, name=f"grouped{a}", align_bytes=64) for a in range(PASSES)]
 
         def cast(copy, a, lo, hi):
-            copy(grouped[a][:, lo:hi, :], raw[a][:].rearrange("p j t -> p t j")[:, lo:hi, :])
+            copy(
+                grouped[a][:, lo:hi, :].rearrange("p (c i) j -> p c j i", i=4),
+                raw[a][:, :, lo:hi].rearrange("p j (c i) -> p c j i", i=4),
+            )
 
         def quantize(a, lo, hi):
             nc.vector.quantize_mx(
@@ -92,8 +99,7 @@ def tile_routed_moe_kernel(tc, xT, w_words, w_scales, gate, offs, pos1, pos2, ou
         words0 = keep.tile([P, SLOTS], I32, name="words0", align_bytes=64)
         nc.vector.tensor_copy(words0[:].bitcast(U32), codes[0][:].bitcast(U32).indirect(offs_t[:]))
         cast(nc.scalar.copy, 1, 0, HALF)
-        cast(nc.scalar.copy, 1, HALF, SCALAR_TOKENS[1])
-        cast(nc.vector.tensor_copy, 1, SCALAR_TOKENS[1], T)
+        cast(nc.scalar.copy, 1, HALF, T)
         quantize(1, 0, HALF)
         quantize(1, HALF, T)
 
@@ -120,21 +126,25 @@ def tile_routed_moe_kernel(tc, xT, w_words, w_scales, gate, offs, pos1, pos2, ou
 
         u_words1 = words1[:].bitcast(U32)
         u_codes1 = codes[1][:].bitcast(U32)
-        acc = {}
-
         def open_groups(experts):
             for e in experts:
-                for b in range(2):
-                    acc_t = psum.tile([P, C], F32, name="acc")
-                    multiply(acc_t, 0, e, b, 0)
-                    acc[e, b] = acc_t
+                acc[e] = psum.tile([P, C], F32, name="acc_t", tag="acc")
+                multiply(acc[e], 0, e, 0, 0)
 
         def close_groups(experts):
-            for b in range(2):
-                for e in experts:
-                    multiply(acc[e, b], 0, e, b, 1)
-                    nc.scalar.copy(y[b][:, e * C : (e + 1) * C], acc[e, b][:])
+            for e in experts:
+                multiply(acc[e], 0, e, 0, 1)
+                nc.scalar.copy(y[0][:, e * C : (e + 1) * C], acc[e][:])
 
+        def second_block(experts):
+            bank = psum.tile([P, len(experts) * C], F32, name="bank", tag="acc")
+            lo = experts[0]
+            for e in experts:
+                for a in range(PASSES):
+                    multiply(bank, (e - lo) * C, e, 1, a)
+            nc.scalar.copy(y[1][:, lo * C : (lo + len(experts)) * C], bank[:])
+
+        acc = {}
         gather(byte_t, scales, 0, 512)
         open_groups(range(0, 4))
         gather(u_words1, u_codes1, 0, 256)
@@ -142,16 +152,13 @@ def tile_routed_moe_kernel(tc, xT, w_words, w_scales, gate, offs, pos1, pos2, ou
         gather(u_words1, u_codes1, 256, 512)
         close_groups(range(2, 4))
         gather(byte_t, scales, 512, 1024)
-        open_groups(range(4, 6))
+        open_groups(range(4, 8))
         gather(u_words1, u_codes1, 512, 768)
         close_groups(range(4, 6))
         gather(u_words1, u_codes1, 768, 1024)
-        for b in range(2):
-            acc_t = psum.tile([P, 2 * C], F32, name="acc")
-            for e in (6, 7):
-                for a in range(PASSES):
-                    multiply(acc_t, (e - 6) * C, e, b, a)
-            nc.scalar.copy(y[b][:, 6 * C :], acc_t[:])
+        close_groups(range(6, 8))
+        second_block(range(0, 4))
+        second_block(range(4, 8))
 
         first = [keep.tile([P, T], F32, name=f"first{b}") for b in range(2)]
         second = [keep.tile([P, T], F32, name=f"second{b}") for b in range(2)]

from contextlib import ExitStack

import concourse.mybir as mybir
from concourse.masks import make_identity

K, T, E, C, N = 1024, 512, 8, 128, 256
P = 128
PASSES = K // 512
SLOTS = E * C
HALF = T // 2
WINDOW = 1536
FLOPS = 2 * K * N * SLOTS

F32 = mybir.dt.float32
BF16 = mybir.dt.bfloat16
I32 = mybir.dt.int32
U32 = mybir.dt.uint32
U16 = mybir.dt.uint16
U8 = mybir.dt.uint8
FP8X4 = mybir.dt.float8_e4m3fn_x4
MULT = mybir.AluOpType.mult
ADD = mybir.AluOpType.add

SCALAR_TOKENS = [168]


def tile_routed_moe_kernel(tc, xT, w_words, w_scales, gate, offs, pos1, pos2, out):
    nc = tc.nc
    x_rows = xT.rearrange("(a p j) t -> a p j t", p=P, j=4)
    w_rows = w_words.rearrange("e a p n r -> p (e a) (n r)")
    ws_rows = w_scales.rearrange("e a (q r) n -> r q (e a) n", r=4)

    with ExitStack() as ctx:
        lists = ctx.enter_context(tc.tile_pool(name="lists", bufs=1))
        keep = ctx.enter_context(tc.tile_pool(name="keep", bufs=1))
        psum = ctx.enter_context(tc.psum_pool(name="psum", bufs=8))

        offs_t = lists.tile([P, SLOTS // 16], U16, name="offs_t")
        pos1_t = lists.tile([P, T // 16], U16, name="pos1_t")
        pos2_t = lists.tile([P, T // 16], U16, name="pos2_t")

        codes = [keep.tile([P, WINDOW], I32, name=f"codes{a}", align_bytes=64) for a in range(PASSES)]
        scales = keep.tile([P, WINDOW], U8, name="scales", align_bytes=64)
        ws = keep.tile([P, E * PASSES, N], U8, name="ws", align_bytes=64)
        nc.gpsimd.memset(scales[:].bitcast(I32), 0)
        nc.gpsimd.memset(ws[:].rearrange("p g n -> p (g n)").bitcast(I32), 0)
        ident = keep.tile([P, P], F32, name="ident")
        make_identity(nc, ident[:])
        for a in range(PASSES):
            nc.vector.memset(codes[a][:, T:], 0)

        raw = []
        for a in range(PASSES):
            r_t = keep.tile([P, 4, T], F32, name=f"raw{a}")
            if a == 0:
                nc.sync.dma_start(r_t[:], x_rows[a])
            else:
                for h in range(2):
                    nc.sync.dma_start(r_t[:, :, h * HALF : (h + 1) * HALF], x_rows[a, :, :, h * HALF : (h + 1) * HALF])
            raw.append(r_t)
            if a == 0:
                nc.sync.dma_start(offs_t[:], offs)
        for r in range(4):
            nc.sync.dma_start(ws[r:P:32, :, :].bitcast(I32), ws_rows[r].bitcast(I32))
        ww = []
        for h in range(4):
            w_t = keep.tile([P, E * PASSES // 4, N], I32, name=f"ww{h}", align_bytes=64)
            nc.sync.dma_start(w_t[:], w_rows[:, 4 * h : 4 * h + 4, :].bitcast(I32))
            ww.append(w_t)
        nc.sync.dma_start(pos1_t[:], pos1)
        nc.sync.dma_start(pos2_t[:], pos2)
        gates = {}
        for b in range(2):
            for r in range(2):
                g_t = keep.tile([P, T], F32, name=f"gate{r}{b}")
                nc.sync.dma_start(g_t[:], gate[r, b * P : (b + 1) * P, :])
                gates[r, b] = g_t

        grouped = [keep.tile([P, T, 4], BF16, name=f"grouped{a}", align_bytes=64) for a in range(PASSES)]

        def cast(copy, a, lo, hi):
            copy(
                grouped[a][:, lo:hi, :].rearrange("p (c i) j -> p c j i", i=4),
                raw[a][:, :, lo:hi].rearrange("p j (c i) -> p c j i", i=4),
            )

        def quantize(a, lo, hi):
            nc.vector.quantize_mx(
                out=codes[a][:, lo:hi].bitcast(FP8X4),
                scales=scales[4 * a : P, lo:hi],
                in_=grouped[a][:, lo:hi, :].rearrange("p t j -> p (t j)"),
            )

        cast(nc.scalar.copy, 0, 0, SCALAR_TOKENS[0])
        cast(nc.vector.tensor_copy, 0, HALF, T)
        cast(nc.vector.tensor_copy, 0, SCALAR_TOKENS[0], HALF)
        quantize(0, HALF, T)
        quantize(0, 0, HALF)
        words0 = keep.tile([P, SLOTS], I32, name="words0", align_bytes=64)
        nc.vector.tensor_copy(words0[:].bitcast(U32), codes[0][:].bitcast(U32).indirect(offs_t[:]))
        cast(nc.scalar.copy, 1, 0, HALF)
        cast(nc.scalar.copy, 1, HALF, T)
        quantize(1, 0, HALF)
        quantize(1, HALF, T)

        y = [keep.tile([P, SLOTS], F32, name=f"y{b}") for b in range(2)]
        byte_t = keep.tile([P, SLOTS], U8, name="byte_t", align_bytes=64)
        words1 = keep.tile([P, SLOTS], I32, name="words1", align_bytes=64)

        def gather(dst, src, lo, hi):
            window = 1024 if hi - lo > 256 else 512
            nc.vector.tensor_copy(dst[:, lo:hi], src[:, :window].indirect(offs_t[:, lo // 16 : hi // 16]))

        def multiply(acc, c0, e, b, a):
            slots = slice(e * C, (e + 1) * C)
            words = words0 if a == 0 else words1
            nc.tensor.matmul_mx(
                out=acc[:, c0 : c0 + C],
                lhsT=ww[e // 2][:, (e % 2) * PASSES + a, b * P : (b + 1) * P].bitcast(FP8X4),
                lhsT_scale=ws[:, e * PASSES + a, b * P : (b + 1) * P],
                rhs=words[:, slots].bitcast(FP8X4),
                rhs_scale=byte_t[4 * a : P, slots],
                start=(a == 0),
                stop=(a == PASSES - 1),
            )

        u_words1 = words1[:].bitcast(U32)
        u_codes1 = codes[1][:].bitcast(U32)
        def open_groups(experts):
            for e in experts:
                acc[e] = psum.tile([P, C], F32, name="acc_t", tag="acc")
                multiply(acc[e], 0, e, 0, 0)

        def close_groups(experts):
            for e in experts:
                multiply(acc[e], 0, e, 0, 1)
                nc.scalar.copy(y[0][:, e * C : (e + 1) * C], acc[e][:])

        def second_block(experts):
            bank = psum.tile([P, len(experts) * C], F32, name="bank", tag="acc")
            lo = experts[0]
            for e in experts:
                for a in range(PASSES):
                    multiply(bank, (e - lo) * C, e, 1, a)
            nc.scalar.copy(y[1][:, lo * C : (lo + len(experts)) * C], bank[:])

        acc = {}
        gather(byte_t, scales, 0, 512)
        open_groups(range(0, 4))
        gather(u_words1, u_codes1, 0, 256)
        close_groups(range(0, 2))
        gather(u_words1, u_codes1, 256, 512)
        close_groups(range(2, 4))
        gather(byte_t, scales, 512, 1024)
        open_groups(range(4, 8))
        gather(u_words1, u_codes1, 512, 768)
        close_groups(range(4, 6))
        gather(u_words1, u_codes1, 768, 1024)
        close_groups(range(6, 8))
        second_block(range(0, 4))
        second_block(range(4, 8))

        first = [keep.tile([P, T], F32, name=f"first{b}") for b in range(2)]
        second = [keep.tile([P, T], F32, name=f"second{b}") for b in range(2)]
        both = psum.tile([P, 256], F32, name="both", tag="acc")
        summed = keep.tile([P, 256], F32, name="summed")
        for b in range(2):
            nc.vector.tensor_tensor(first[b][:], y[b][:].indirect(pos1_t[:]), gates[0, b][:], MULT)
            nc.vector.tensor_tensor(second[b][:], y[b][:].indirect(pos2_t[:]), gates[1, b][:], MULT)
            if b == 0:
                nc.tensor.matmul(both[:], ident[:], first[0][:, :256], start=True, stop=False)
                nc.tensor.matmul(both[:], ident[:], second[0][:, :256], start=False, stop=True)
                nc.scalar.copy(summed[:], both[:])
                nc.sync.dma_start(out[:P, :256], summed[:])
        nc.vector.tensor_tensor(second[0][:, 256:], first[0][:, 256:], second[0][:, 256:], ADD)
        nc.sync.dma_start(out[:P, 256:], second[0][:, 256:])
        for h in range(2):
            cols = slice(h * HALF, (h + 1) * HALF)
            nc.vector.tensor_tensor(second[1][:, cols], first[1][:, cols], second[1][:, cols], ADD)
            nc.sync.dma_start(out[P:, cols], second[1][:, cols])
